import numpy as np
import ml_dtypes


def mxq(x, axis, fmt="e4m3"):
    dtype, down = {"e4m3": (ml_dtypes.float8_e4m3fn, 7), "e5m2": (ml_dtypes.float8_e5m2, 14)}[fmt]
    v = np.moveaxis(np.asarray(x, np.float32).astype(ml_dtypes.bfloat16).astype(np.float64), axis, -1)
    blocks = v.reshape(v.shape[:-1] + (-1, 32))
    amax = np.abs(blocks).max(-1, keepdims=True)
    byte = np.maximum(np.where(amax > 0, np.frexp(amax)[1] - 1 + 127, 0) - down, 1)
    scale = np.exp2(byte - 127.0)
    codes = (blocks / scale).astype(np.float32).astype(dtype).astype(np.float64)
    return np.moveaxis((codes * scale).reshape(v.shape), -1, axis)


WIDE = False


def mx_kscale(k):
    if not WIDE:
        return np.ones(k)
    levels = np.array([10, -10, 5, -5, 0])
    if k % 512:
        return np.exp2(np.random.permutation(np.resize(levels, k // 32))).repeat(32)
    a = np.empty((k // 512, 16))
    for p in range(k // 512):
        a[p, :8] = np.random.permutation(np.resize(levels, 8))
        for g in range(8):
            far = levels[np.abs(levels - a[p, g]) >= 10]
            a[p, g + 8] = far[np.random.randint(len(far))]
    return np.exp2(a.ravel()).repeat(32)


def f64(x):
    return np.asarray(x).astype(np.float64)


def striped(idx):
    return np.tile(np.asarray(idx).reshape(-1, 16).T, (8, 1)).astype(np.uint16)


def unstriped(offs):
    return offs[:16].T.reshape(-1).astype(np.int64)


E2M1 = np.array([0.0, 0.5, 1.0, 1.5, 2.0, 3.0, 4.0, 6.0, -0.0, -0.5, -1.0, -1.5, -2.0, -3.0, -4.0, -6.0])


def pack_weight(w, fmt):
    k, n = w.shape
    w = f64(np.asarray(w, np.float32).astype(ml_dtypes.bfloat16)).reshape(k // 32, 32, n)
    amax = np.abs(w).max(1)
    if fmt == "e4m3":
        byte = np.frexp(amax)[1] - 1 + 127 - 7
    else:
        mant, ex = np.frexp(amax / 6.0)
        byte = np.where(mant > 0.5, ex, ex - 1) + 127
    byte = np.clip(np.where(amax > 0, byte, 1), 1, 254)
    scaled = (w * np.exp2(127.0 - byte)[:, None, :]).reshape(k, n).astype(np.float32)
    by_word = np.ascontiguousarray(scaled.reshape(k // 512, 128, 4, n).transpose(0, 1, 3, 2))
    if fmt == "e4m3":
        words = by_word.astype(ml_dtypes.float8_e4m3fn).view(np.uint8)
    else:
        c = by_word.astype(ml_dtypes.float4_e2m1fn).view(np.uint8) & 0xF
        words = (c[..., 0::2] | (c[..., 1::2] << 4)).reshape(k // 512, 128, 2 * n)
    return np.ascontiguousarray(words), np.ascontiguousarray(byte.astype(np.uint8).reshape(k // 512, 16, n))


def unpack_weight(words, scales, fmt):
    g, _, n = scales.shape
    words = np.ascontiguousarray(words).reshape(g, 128, n, -1)
    if fmt == "e4m3":
        vals = words.view(ml_dtypes.float8_e4m3fn).astype(np.float64)
    else:
        nib = np.empty((g, 128, n, 4), np.uint8)
        nib[..., 0::2] = words & 0xF
        nib[..., 1::2] = words >> 4
        vals = E2M1[nib]
    vals = vals * np.repeat(np.exp2(scales.astype(np.float64) - 127.0), 8, axis=1)[..., None]
    return vals.transpose(0, 1, 3, 2).reshape(g * 512, n)


D, C, T, I, Q = 512, 512, 2048, 512, 256


def setup_inputs():
    n = np.random.standard_normal
    idx = np.random.permutation(T)[:I]
    fd = mx_kscale(D)
    fc = mx_kscale(C)
    latp = pack_weight(n((C, T)) / fc[:, None], "e4m3")
    return {
        "query": (n((D, Q)) * 1.0 / np.sqrt(D) * fd[:, None]).astype(np.float32),
        "wuk": (n((D, C)) * 0.8 / np.sqrt(D) / fd[:, None] * fc).astype(np.float32),
        "lat_words": latp[0],
        "lat_scales": latp[1],
        "offs": striped(idx),
    }


def reference(query, wuk, lat_words, lat_scales, offs):
    idx = unstriped(offs)
    latu = unpack_weight(lat_words, lat_scales, "e4m3")
    wukq = mxq(f64(wuk), 0, "e4m3")
    queryq = mxq(f64(query), 0, "e4m3")
    b = wukq.T @ queryq
    bq = mxq(b, 0, "e4m3")
    latidxg = latu[:, idx]
    a = bq.T @ latidxg
    p = np.exp(a - np.max(a, axis=1, keepdims=True))
    y = p / np.sum(p, axis=1, keepdims=True) * 512.0
    return y

@@ -1,0 +1,121 @@
+from contextlib import ExitStack
+
+import concourse.mybir as mybir
+
+D, C, T, I, Q = 512, 512, 2048, 512, 256
+FLOPS = 2 * D * C * Q + 2 * C * Q * I
+
+F32 = mybir.dt.float32
+BF16 = mybir.dt.bfloat16
+I32 = mybir.dt.int32
+U32 = mybir.dt.uint32
+U16 = mybir.dt.uint16
+U8 = mybir.dt.uint8
+FP8X4 = mybir.dt.float8_e4m3fn_x4
+ALU = mybir.AluOpType
+ACT = mybir.ActivationFunctionType
+AXIS = mybir.AxisListType
+
+P = 128
+PACK = 4
+HALF = I // 2
+M_VECTOR = 88
+
+
+def tile_attend_absorbscores_kernel(tc, query, wuk, lat_words, lat_scales, offs, out):
+    nc = tc.nc
+    with ExitStack() as ctx:
+        keep = ctx.enter_context(tc.tile_pool(name="keep", bufs=1))
+        psum = ctx.enter_context(tc.psum_pool(name="psum", bufs=1))
+
+        offsets = keep.tile([P, I // 16], U16, name="offsets")
+        nc.sync.dma_start(offsets[:], offs)
+
+        w_raw = keep.tile([P, PACK, C], F32, name="w_raw")
+        nc.sync.dma_start(w_raw[:], wuk.rearrange("(p j) c -> p j c", j=PACK))
+        q_raw = keep.tile([P, PACK, Q], F32, name="q_raw")
+        nc.sync.dma_start(q_raw[:], query.rearrange("(p j) q -> p j q", j=PACK))
+        lat_w = keep.tile([P, T], U32, name="lat_w", align_bytes=64)
+        nc.sync.dma_start(lat_w[:].bitcast(I32), lat_words[0].rearrange("p n t -> p (n t)").bitcast(I32))
+
+        lat_s = keep.tile([P, T], U8, name="lat_s", align_bytes=64)
+        nc.vector.memset(lat_s[:].bitcast(I32), 0)
+        for g in range(4):
+            nc.scalar.dma_start(lat_s[32 * g : 32 * g + 4, :].bitcast(I32), lat_scales[0, 4 * g : 4 * g + 4, :].bitcast(I32))
+
+        warm_in = keep.tile([P, 1], F32, name="warm_in")
+        warm_out = keep.tile([P, 1], F32, name="warm_out")
+        nc.vector.memset(warm_in[:], 0.0)
+        nc.scalar.activation(warm_out[:], warm_in[:], ACT.Exp)
+
+        key_s = keep.tile([P, I], U8, name="key_s", align_bytes=64)
+        nc.vector.tensor_copy(key_s[:], lat_s[:].indirect(offsets[:]))
+
+        w_bf = keep.tile([P, PACK, P, PACK], BF16, name="w_bf", align_bytes=64)
+        w_src = w_raw[:].rearrange("p j (m t) -> p m t j", t=PACK)
+        w_dst = w_bf[:].rearrange("p t m j -> p m t j")
+        nc.vector.tensor_copy(w_dst[:, :M_VECTOR], w_src[:, :M_VECTOR])
+        nc.scalar.copy(w_dst[:, M_VECTOR:], w_src[:, M_VECTOR:])
+        w_codes = keep.tile([P, C], U32, name="w_codes", align_bytes=64)
+        w_scales = keep.tile([P, C], U8, name="w_scales", align_bytes=64)
+        nc.vector.quantize_mx(out=w_codes[:].bitcast(FP8X4), scales=w_scales[:], in_=w_bf[:].rearrange("p t m j -> p (t m j)"))
+
+        b_codes = []
+        b_scales = []
+        for h in range(2):
+            cols = slice(h * P, (h + 1) * P)
+            q_bf = keep.tile([P, P, PACK], BF16, name="q_bf%d" % h, tag="shared%d" % h, align_bytes=64)
+            nc.scalar.copy(
+                q_bf[:].rearrange("p (c i) j -> p c j i", i=4),
+                q_raw[:, :, cols].rearrange("p j (c i) -> p c j i", i=4),
+            )
+            q_codes = keep.tile([P, P], U32, name="q_codes%d" % h, align_bytes=64)
+            q_scales = keep.tile([P, P], U8, name="q_scales%d" % h, align_bytes=64)
+            nc.vector.quantize_mx(out=q_codes[:].bitcast(FP8X4), scales=q_scales[:], in_=q_bf[:].rearrange("p q j -> p (q j)"))
+            b_ps = psum.tile([P, PACK, P], F32, name="b_ps%d" % h)
+            for t in range(PACK):
+                wc = slice(t * P, (t + 1) * P)
+                nc.tensor.matmul_mx(
+                    out=b_ps[:, t, :],
+                    lhsT=w_codes[:, wc].bitcast(FP8X4),
+                    lhsT_scale=w_scales[:, wc],
+                    rhs=q_codes[:].bitcast(FP8X4),
+                    rhs_scale=q_scales[:],
+                    start=True,
+                    stop=True,
+                )
+            b_bf = keep.tile([P, P, PACK], BF16, name="b_bf%d" % h, tag="b_bf%d" % h, align_bytes=64)
+            nc.scalar.copy(b_bf[:], b_ps[:].rearrange("p t q -> p q t"))
+            codes = keep.tile([P, P], U32, name="b_codes%d" % h, align_bytes=64)
+            scales = keep.tile([P, P], U8, name="b_scales%d" % h, align_bytes=64)
+            nc.vector.quantize_mx(out=codes[:].bitcast(FP8X4), scales=scales[:], in_=b_bf[:].rearrange("p q t -> p (q t)"))
+            b_codes.append(codes)
+            b_scales.append(scales)
+
+        scores = [psum.tile([P, I], F32, name="scores%d" % h) for h in range(2)]
+        for u in range(2):
+            slots = slice(u * HALF, (u + 1) * HALF)
+            key_w = keep.tile([P, HALF], U32, name="key_w%d" % u, tag=("shared1", "b_bf0")[u], align_bytes=64)
+            nc.vector.tensor_copy(key_w[:], lat_w[:].indirect(offsets[:, u * (HALF // 16) : (u + 1) * (HALF // 16)]))
+            for h in range(2):
+                nc.tensor.matmul_mx(
+                    out=scores[h][:, slots],
+                    lhsT=b_codes[h][:].bitcast(FP8X4),
+                    lhsT_scale=b_scales[h][:],
+                    rhs=key_w[:].bitcast(FP8X4),
+                    rhs_scale=key_s[:, slots],
+                    start=True,
+                    stop=True,
+                )
+
+        for h in range(2):
+            neg_max = keep.tile([P, 1], F32, name="neg_max%d" % h)
+            nc.vector.tensor_reduce(neg_max[:], scores[h][:], AXIS.X, ALU.max, negate=True)
+            p = keep.tile([P, I], F32, name="p%d" % h)
+            total = keep.tile([P, 1], F32, name="total%d" % h)
+            nc.scalar.activation(p[:], scores[h][:], ACT.Exp, bias=neg_max[:], scale=1.0, accum_out=total[:])
+            inv = keep.tile([P, 1], F32, name="inv%d" % h)
+            nc.vector.reciprocal(inv[:], total[:])
+            y = keep.tile([P, I], F32, name="y%d" % h)
+            nc.vector.tensor_scalar(y[:], p[:], inv[:], 512.0, ALU.mult, ALU.mult)
+            nc.sync.dma_start(out[h * P : (h + 1) * P, :], y[:])

@@ -28,28 +28,19 @@ def tile_attend_absorbscores_kernel(tc, query, wuk, lat_words, lat_scales, offs,
         keep = ctx.enter_context(tc.tile_pool(name="keep", bufs=1))
         psum = ctx.enter_context(tc.psum_pool(name="psum", bufs=1))
 
+        lat_s = keep.tile([P, T], U8, name="lat_s", tag="lat_s", align_bytes=64)
+        nc.vector.memset(lat_s[:].bitcast(I32), 0)
+
         offsets = keep.tile([P, I // 16], U16, name="offsets")
         nc.sync.dma_start(offsets[:], offs)
-
         w_raw = keep.tile([P, PACK, C], F32, name="w_raw")
         nc.sync.dma_start(w_raw[:], wuk.rearrange("(p j) c -> p j c", j=PACK))
         q_raw = keep.tile([P, PACK, Q], F32, name="q_raw")
         nc.sync.dma_start(q_raw[:], query.rearrange("(p j) q -> p j q", j=PACK))
-        lat_w = keep.tile([P, T], U32, name="lat_w", align_bytes=64)
-        nc.sync.dma_start(lat_w[:].bitcast(I32), lat_words[0].rearrange("p n t -> p (n t)").bitcast(I32))
-
-        lat_s = keep.tile([P, T], U8, name="lat_s", align_bytes=64)
-        nc.vector.memset(lat_s[:].bitcast(I32), 0)
         for g in range(4):
-            nc.scalar.dma_start(lat_s[32 * g : 32 * g + 4, :].bitcast(I32), lat_scales[0, 4 * g : 4 * g + 4, :].bitcast(I32))
-
-        warm_in = keep.tile([P, 1], F32, name="warm_in")
-        warm_out = keep.tile([P, 1], F32, name="warm_out")
-        nc.vector.memset(warm_in[:], 0.0)
-        nc.scalar.activation(warm_out[:], warm_in[:], ACT.Exp)
-
-        key_s = keep.tile([P, I], U8, name="key_s", align_bytes=64)
-        nc.vector.tensor_copy(key_s[:], lat_s[:].indirect(offsets[:]))
+            nc.sync.dma_start(lat_s[32 * g : 32 * g + 4, :].bitcast(I32), lat_scales[0, 4 * g : 4 * g + 4, :].bitcast(I32))
+        lat_w = keep.tile([P, T], U32, name="lat_w", tag="lat_w", align_bytes=64)
+        nc.sync.dma_start(lat_w[:].bitcast(I32), lat_words[0].rearrange("p n t -> p (n t)").bitcast(I32))
 
         w_bf = keep.tile([P, PACK, P, PACK], BF16, name="w_bf", align_bytes=64)
         w_src = w_raw[:].rearrange("p j (m t) -> p m t j", t=PACK)
@@ -60,23 +51,23 @@ def tile_attend_absorbscores_kernel(tc, query, wuk, lat_words, lat_scales, offs,
         w_scales = keep.tile([P, C], U8, name="w_scales", align_bytes=64)
         nc.vector.quantize_mx(out=w_codes[:].bitcast(FP8X4), scales=w_scales[:], in_=w_bf[:].rearrange("p t m j -> p (t m j)"))
 
-        b_codes = []
-        b_scales = []
+        halves = [offsets[:, u * (HALF // 16) : (u + 1) * (HALF // 16)] for u in range(2)]
+        b_ps = []
         for h in range(2):
             cols = slice(h * P, (h + 1) * P)
-            q_bf = keep.tile([P, P, PACK], BF16, name="q_bf%d" % h, tag="shared%d" % h, align_bytes=64)
+            q_bf = keep.tile([P, P, PACK], BF16, name="q_bf%d" % h, tag="q_bf%d" % h, align_bytes=64)
             nc.scalar.copy(
                 q_bf[:].rearrange("p (c i) j -> p c j i", i=4),
                 q_raw[:, :, cols].rearrange("p j (c i) -> p c j i", i=4),
             )
-            q_codes = keep.tile([P, P], U32, name="q_codes%d" % h, align_bytes=64)
+            q_codes = keep.tile([P, P], U32, name="q_codes%d" % h, tag=("q_codes0", "lat_s")[h], align_bytes=64)
             q_scales = keep.tile([P, P], U8, name="q_scales%d" % h, align_bytes=64)
             nc.vector.quantize_mx(out=q_codes[:].bitcast(FP8X4), scales=q_scales[:], in_=q_bf[:].rearrange("p q j -> p (q j)"))
-            b_ps = psum.tile([P, PACK, P], F32, name="b_ps%d" % h)
+            bank = psum.tile([P, PACK, P], F32, name="b_ps%d" % h)
             for t in range(PACK):
                 wc = slice(t * P, (t + 1) * P)
                 nc.tensor.matmul_mx(
-                    out=b_ps[:, t, :],
+                    out=bank[:, t, :],
                     lhsT=w_codes[:, wc].bitcast(FP8X4),
                     lhsT_scale=w_scales[:, wc],
                     rhs=q_codes[:].bitcast(FP8X4),
@@ -84,25 +75,37 @@ def tile_attend_absorbscores_kernel(tc, query, wuk, lat_words, lat_scales, offs,
                     start=True,
                     stop=True,
                 )
+            b_ps.append(bank)
+            if h == 0:
+                key_s = keep.tile([P, I], U8, name="key_s", align_bytes=64)
+                nc.vector.tensor_copy(key_s[:], lat_s[:].indirect(offsets[:]))
+
+        key_w = []
+        b_codes = []
+        b_scales = []
+        for h in range(2):
+            if h == 1:
+                for u in range(2):
+                    gathered = keep.tile([P, HALF], U32, name="key_w%d" % u, align_bytes=64)
+                    nc.vector.tensor_copy(gathered[:], lat_w[:].indirect(halves[u]))
+                    key_w.append(gathered)
             b_bf = keep.tile([P, P, PACK], BF16, name="b_bf%d" % h, tag="b_bf%d" % h, align_bytes=64)
-            nc.scalar.copy(b_bf[:], b_ps[:].rearrange("p t q -> p q t"))
-            codes = keep.tile([P, P], U32, name="b_codes%d" % h, align_bytes=64)
+            nc.scalar.copy(b_bf[:], b_ps[h][:].rearrange("p t q -> p q t"))
+            codes = keep.tile([P, P], U32, name="b_codes%d" % h, tag=("b_codes0", "lat_w")[h], align_bytes=64)
             scales = keep.tile([P, P], U8, name="b_scales%d" % h, align_bytes=64)
             nc.vector.quantize_mx(out=codes[:].bitcast(FP8X4), scales=scales[:], in_=b_bf[:].rearrange("p q t -> p (q t)"))
             b_codes.append(codes)
             b_scales.append(scales)
 
         scores = [psum.tile([P, I], F32, name="scores%d" % h) for h in range(2)]
-        for u in range(2):
-            slots = slice(u * HALF, (u + 1) * HALF)
-            key_w = keep.tile([P, HALF], U32, name="key_w%d" % u, tag=("shared1", "b_bf0")[u], align_bytes=64)
-            nc.vector.tensor_copy(key_w[:], lat_w[:].indirect(offsets[:, u * (HALF // 16) : (u + 1) * (HALF // 16)]))
-            for h in range(2):
+        for h in range(2):
+            for u in range(2):
+                slots = slice(u * HALF, (u + 1) * HALF)
                 nc.tensor.matmul_mx(
                     out=scores[h][:, slots],
                     lhsT=b_codes[h][:].bitcast(FP8X4),
                     lhsT_scale=b_scales[h][:],
-                    rhs=key_w[:].bitcast(FP8X4),
+                    rhs=key_w[u][:].bitcast(FP8X4),
                     rhs_scale=key_s[:, slots],
                     start=True,
                     stop=True,
@@ -116,6 +119,12 @@ def tile_attend_absorbscores_kernel(tc, query, wuk, lat_words, lat_scales, offs,
             nc.scalar.activation(p[:], scores[h][:], ACT.Exp, bias=neg_max[:], scale=1.0, accum_out=total[:])
             inv = keep.tile([P, 1], F32, name="inv%d" % h)
             nc.vector.reciprocal(inv[:], total[:])
-            y = keep.tile([P, I], F32, name="y%d" % h)
-            nc.vector.tensor_scalar(y[:], p[:], inv[:], 512.0, ALU.mult, ALU.mult)
-            nc.sync.dma_start(out[h * P : (h + 1) * P, :], y[:])
+            rows = slice(h * P, (h + 1) * P)
+            pieces = 1 + h
+            width = I // pieces
+            for v in range(pieces):
+                part = slice(v * width, (v + 1) * width)
+                y = keep.tile([P, width], F32, name="y%d_%d" % (h, v))
+                nc.vector.tensor_scalar(y[:], p[:, part], inv[:], 512.0, ALU.mult, ALU.mult)
+                queue = nc.scalar if v else nc.sync
+                queue.dma_start(out[rows, part], y[:])

@@ -19,24 +19,25 @@ AXIS = mybir.AxisListType
 P = 128
 PACK = 4
 HALF = I // 2
-M_VECTOR = 88
+M_VECTOR = 84
 
 
 def tile_attend_absorbscores_kernel(tc, query, wuk, lat_words, lat_scales, offs, out):
     nc = tc.nc
     with ExitStack() as ctx:
         keep = ctx.enter_context(tc.tile_pool(name="keep", bufs=1))
+        reuse = ctx.enter_context(tc.tile_pool(name="reuse", bufs=1))
         psum = ctx.enter_context(tc.psum_pool(name="psum", bufs=1))
 
-        lat_s = keep.tile([P, T], U8, name="lat_s", tag="lat_s", align_bytes=64)
+        lat_s = reuse.tile([P, T], U8, name="lat_s", align_bytes=64, offset=0)
         nc.vector.memset(lat_s[:].bitcast(I32), 0)
 
-        offsets = keep.tile([P, I // 16], U16, name="offsets")
-        nc.sync.dma_start(offsets[:], offs)
         w_raw = keep.tile([P, PACK, C], F32, name="w_raw")
         nc.sync.dma_start(w_raw[:], wuk.rearrange("(p j) c -> p j c", j=PACK))
         q_raw = keep.tile([P, PACK, Q], F32, name="q_raw")
         nc.sync.dma_start(q_raw[:], query.rearrange("(p j) q -> p j q", j=PACK))
+        offsets = keep.tile([P, I // 16], U16, name="offsets")
+        nc.sync.dma_start(offsets[:], offs)
         for g in range(4):
             nc.sync.dma_start(lat_s[32 * g : 32 * g + 4, :].bitcast(I32), lat_scales[0, 4 * g : 4 * g + 4, :].bitcast(I32))
         lat_w = keep.tile([P, T], U32, name="lat_w", tag="lat_w", align_bytes=64)
@@ -60,7 +61,10 @@ def tile_attend_absorbscores_kernel(tc, query, wuk, lat_words, lat_scales, offs,
                 q_bf[:].rearrange("p (c i) j -> p c j i", i=4),
                 q_raw[:, :, cols].rearrange("p j (c i) -> p c j i", i=4),
             )
-            q_codes = keep.tile([P, P], U32, name="q_codes%d" % h, tag=("q_codes0", "lat_s")[h], align_bytes=64)
+            if h == 0:
+                q_codes = keep.tile([P, P], U32, name="q_codes0", align_bytes=64)
+            else:
+                q_codes = reuse.tile([P, P], U32, name="q_codes1", align_bytes=64, offset=0)
             q_scales = keep.tile([P, P], U8, name="q_scales%d" % h, align_bytes=64)
             nc.vector.quantize_mx(out=q_codes[:].bitcast(FP8X4), scales=q_scales[:], in_=q_bf[:].rearrange("p q j -> p (q j)"))
             bank = psum.tile([P, PACK, P], F32, name="b_ps%d" % h)
@@ -91,7 +95,10 @@ def tile_attend_absorbscores_kernel(tc, query, wuk, lat_words, lat_scales, offs,
                     key_w.append(gathered)
             b_bf = keep.tile([P, P, PACK], BF16, name="b_bf%d" % h, tag="b_bf%d" % h, align_bytes=64)
             nc.scalar.copy(b_bf[:], b_ps[h][:].rearrange("p t q -> p q t"))
-            codes = keep.tile([P, P], U32, name="b_codes%d" % h, tag=("b_codes0", "lat_w")[h], align_bytes=64)
+            if h == 0:
+                codes = reuse.tile([P, P], U32, name="b_codes0", align_bytes=64, offset=512)
+            else:
+                codes = keep.tile([P, P], U32, name="b_codes1", tag="lat_w", align_bytes=64)
             scales = keep.tile([P, P], U8, name="b_scales%d" % h, align_bytes=64)
             nc.vector.quantize_mx(out=codes[:].bitcast(FP8X4), scales=scales[:], in_=b_bf[:].rearrange("p q t -> p (q t)"))
             b_codes.append(codes)

@@ -20,6 +20,8 @@ P = 128
 PACK = 4
 HALF = I // 2
 M_VECTOR = 84
+Q_SCALAR = 48
+SCALE_ROWS = 16
 
 
 def tile_attend_absorbscores_kernel(tc, query, wuk, lat_words, lat_scales, offs, out):
@@ -29,60 +31,75 @@ def tile_attend_absorbscores_kernel(tc, query, wuk, lat_words, lat_scales, offs,
         reuse = ctx.enter_context(tc.tile_pool(name="reuse", bufs=1))
         psum = ctx.enter_context(tc.psum_pool(name="psum", bufs=1))
 
-        lat_s = reuse.tile([P, T], U8, name="lat_s", align_bytes=64, offset=0)
-        nc.vector.memset(lat_s[:].bitcast(I32), 0)
+        def quantise(codes, scales, values):
+            nc.vector.quantize_mx(out=codes[:].bitcast(FP8X4), scales=scales[:], in_=values)
 
+        first_row = P - SCALE_ROWS
+        lat_s = keep.tile([P, T], U8, name="lat_s", align_bytes=64)
+        nc.scalar.dma_start(lat_s[first_row:, :].bitcast(I32), lat_scales[0].bitcast(I32))
+        nc.vector.memset(lat_s[:first_row, :].bitcast(I32), 0)
+        key_s = keep.tile([P, I], U8, name="key_s", align_bytes=64)
+        nc.vector.memset(key_s[:].bitcast(I32), 0)
+
+        offsets = keep.tile([P, I // 16], U16, name="offsets")
+        nc.sync.dma_start(offsets[:], offs)
         w_raw = keep.tile([P, PACK, C], F32, name="w_raw")
         nc.sync.dma_start(w_raw[:], wuk.rearrange("(p j) c -> p j c", j=PACK))
         q_raw = keep.tile([P, PACK, Q], F32, name="q_raw")
         nc.sync.dma_start(q_raw[:], query.rearrange("(p j) q -> p j q", j=PACK))
-        offsets = keep.tile([P, I // 16], U16, name="offsets")
-        nc.sync.dma_start(offsets[:], offs)
-        for g in range(4):
-            nc.sync.dma_start(lat_s[32 * g : 32 * g + 4, :].bitcast(I32), lat_scales[0, 4 * g : 4 * g + 4, :].bitcast(I32))
         lat_w = keep.tile([P, T], U32, name="lat_w", tag="lat_w", align_bytes=64)
         nc.sync.dma_start(lat_w[:].bitcast(I32), lat_words[0].rearrange("p n t -> p (n t)").bitcast(I32))
 
-        w_bf = keep.tile([P, PACK, P, PACK], BF16, name="w_bf", align_bytes=64)
+        picked_s = keep.tile([P, I], U8, name="picked_s", align_bytes=64)
+        nc.vector.tensor_copy(picked_s[:], lat_s[:].indirect(offsets[:]))
+        for g in range(4):
+            rows = slice(first_row + 4 * g, first_row + 4 * g + 4)
+            nc.sync.dma_start(key_s[32 * g : 32 * g + 4, :].bitcast(I32), picked_s[rows, :].bitcast(I32))
+
+        w_bf = reuse.tile([P, PACK, P, PACK], BF16, name="w_bf", align_bytes=64, offset=1024)
         w_src = w_raw[:].rearrange("p j (m t) -> p m t j", t=PACK)
         w_dst = w_bf[:].rearrange("p t m j -> p m t j")
         nc.vector.tensor_copy(w_dst[:, :M_VECTOR], w_src[:, :M_VECTOR])
         nc.scalar.copy(w_dst[:, M_VECTOR:], w_src[:, M_VECTOR:])
-        w_codes = keep.tile([P, C], U32, name="w_codes", align_bytes=64)
-        w_scales = keep.tile([P, C], U8, name="w_scales", align_bytes=64)
-        nc.vector.quantize_mx(out=w_codes[:].bitcast(FP8X4), scales=w_scales[:], in_=w_bf[:].rearrange("p t m j -> p (t m j)"))
+        w_scales = [keep.tile([P, P], U8, name="w_scales%d" % t, align_bytes=64) for t in range(PACK)]
+        w_codes = [keep.tile([P, P], U32, name="w_codes%d" % t, align_bytes=64) for t in range(2)]
+        for t in range(2):
+            quantise(w_codes[t], w_scales[t], w_bf[:, t].rearrange("p m j -> p (m j)"))
+
+        q_src = q_raw[:].rearrange("p j (c i) -> p c j i", i=4)
+        q_bf = [
+            reuse.tile([P, P, PACK], BF16, name="q_bf0", align_bytes=64, offset=0),
+            keep.tile([P, P, PACK], BF16, name="q_bf1", align_bytes=64),
+        ]
+        q_dst = [tile[:].rearrange("p (c i) j -> p c j i", i=4) for tile in q_bf]
+        cut = Q_SCALAR // 4
+        nc.scalar.copy(q_dst[0][:, :cut], q_src[:, :cut])
+        nc.vector.tensor_copy(q_dst[0][:, cut:], q_src[:, cut : P // 4])
+        nc.scalar.copy(q_dst[1], q_src[:, P // 4 :])
+        q_scales = [keep.tile([P, P], U8, name="q_scales%d" % h, align_bytes=64) for h in range(2)]
+        q_codes = [keep.tile([P, P], U32, name="q_codes0", align_bytes=64)]
+        quantise(q_codes[0], q_scales[0], q_bf[0][:].rearrange("p q j -> p (q j)"))
+        for t in range(2, PACK):
+            w_codes.append(reuse.tile([P, P], U32, name="w_codes%d" % t, align_bytes=64, offset=512 * (t - 2)))
+            quantise(w_codes[t], w_scales[t], w_bf[:, t].rearrange("p m j -> p (m j)"))
+        q_codes.append(reuse.tile([P, P], U32, name="q_codes1", align_bytes=64, offset=1024))
+        quantise(q_codes[1], q_scales[1], q_bf[1][:].rearrange("p q j -> p (q j)"))
 
         halves = [offsets[:, u * (HALF // 16) : (u + 1) * (HALF // 16)] for u in range(2)]
         b_ps = []
         for h in range(2):
-            cols = slice(h * P, (h + 1) * P)
-            q_bf = keep.tile([P, P, PACK], BF16, name="q_bf%d" % h, tag="q_bf%d" % h, align_bytes=64)
-            nc.scalar.copy(
-                q_bf[:].rearrange("p (c i) j -> p c j i", i=4),
-                q_raw[:, :, cols].rearrange("p j (c i) -> p c j i", i=4),
-            )
-            if h == 0:
-                q_codes = keep.tile([P, P], U32, name="q_codes0", align_bytes=64)
-            else:
-                q_codes = reuse.tile([P, P], U32, name="q_codes1", align_bytes=64, offset=0)
-            q_scales = keep.tile([P, P], U8, name="q_scales%d" % h, align_bytes=64)
-            nc.vector.quantize_mx(out=q_codes[:].bitcast(FP8X4), scales=q_scales[:], in_=q_bf[:].rearrange("p q j -> p (q j)"))
             bank = psum.tile([P, PACK, P], F32, name="b_ps%d" % h)
             for t in range(PACK):
-                wc = slice(t * P, (t + 1) * P)
                 nc.tensor.matmul_mx(
                     out=bank[:, t, :],
-                    lhsT=w_codes[:, wc].bitcast(FP8X4),
-                    lhsT_scale=w_scales[:, wc],
-                    rhs=q_codes[:].bitcast(FP8X4),
-                    rhs_scale=q_scales[:],
+                    lhsT=w_codes[t][:].bitcast(FP8X4),
+                    lhsT_scale=w_scales[t][:],
+                    rhs=q_codes[h][:].bitcast(FP8X4),
+                    rhs_scale=q_scales[h][:],
                     start=True,
                     stop=True,
                 )
             b_ps.append(bank)
-            if h == 0:
-                key_s = keep.tile([P, I], U8, name="key_s", align_bytes=64)
-                nc.vector.tensor_copy(key_s[:], lat_s[:].indirect(offsets[:]))
 
         key_w = []
         b_codes = []
@@ -93,14 +110,14 @@ def tile_attend_absorbscores_kernel(tc, query, wuk, lat_words, lat_scales, offs,
                     gathered = keep.tile([P, HALF], U32, name="key_w%d" % u, align_bytes=64)
                     nc.vector.tensor_copy(gathered[:], lat_w[:].indirect(halves[u]))
                     key_w.append(gathered)
-            b_bf = keep.tile([P, P, PACK], BF16, name="b_bf%d" % h, tag="b_bf%d" % h, align_bytes=64)
+            b_bf = keep.tile([P, P, PACK], BF16, name="b_bf%d" % h, align_bytes=64)
             nc.scalar.copy(b_bf[:], b_ps[h][:].rearrange("p t q -> p q t"))
             if h == 0:
-                codes = reuse.tile([P, P], U32, name="b_codes0", align_bytes=64, offset=512)
+                codes = keep.tile([P, P], U32, name="b_codes0", align_bytes=64)
             else:
                 codes = keep.tile([P, P], U32, name="b_codes1", tag="lat_w", align_bytes=64)
             scales = keep.tile([P, P], U8, name="b_scales%d" % h, align_bytes=64)
-            nc.vector.quantize_mx(out=codes[:].bitcast(FP8X4), scales=scales[:], in_=b_bf[:].rearrange("p q t -> p (q t)"))
+            quantise(codes, scales, b_bf[:].rearrange("p q t -> p (q t)"))
             b_codes.append(codes)
             b_scales.append(scales)
 

@@ -61,8 +61,9 @@ def tile_attend_absorbscores_kernel(tc, query, wuk, lat_words, lat_scales, offs,
         w_dst = w_bf[:].rearrange("p t m j -> p m t j")
         nc.vector.tensor_copy(w_dst[:, :M_VECTOR], w_src[:, :M_VECTOR])
         nc.scalar.copy(w_dst[:, M_VECTOR:], w_src[:, M_VECTOR:])
-        w_scales = [keep.tile([P, P], U8, name="w_scales%d" % t, align_bytes=64) for t in range(PACK)]
-        w_codes = [keep.tile([P, P], U32, name="w_codes%d" % t, align_bytes=64) for t in range(2)]
+        w_scales = [keep.tile([P, P], U8, name="w_scales%d" % t, align_bytes=64) for t in range(2)]
+        w_all = keep.tile([P, C], U32, name="w_all", align_bytes=64)
+        w_codes = [w_all[:, t * P : (t + 1) * P] for t in range(PACK)]
         for t in range(2):
             quantise(w_codes[t], w_scales[t], w_bf[:, t].rearrange("p m j -> p (m j)"))
 
@@ -80,7 +81,7 @@ def tile_attend_absorbscores_kernel(tc, query, wuk, lat_words, lat_scales, offs,
         q_codes = [keep.tile([P, P], U32, name="q_codes0", align_bytes=64)]
         quantise(q_codes[0], q_scales[0], q_bf[0][:].rearrange("p q j -> p (q j)"))
         for t in range(2, PACK):
-            w_codes.append(reuse.tile([P, P], U32, name="w_codes%d" % t, align_bytes=64, offset=512 * (t - 2)))
+            w_scales.append(reuse.tile([P, P], U8, name="w_scales%d" % t, align_bytes=64, offset=512 * (t - 2)))
             quantise(w_codes[t], w_scales[t], w_bf[:, t].rearrange("p m j -> p (m j)"))
         q_codes.append(reuse.tile([P, P], U32, name="q_codes1", align_bytes=64, offset=1024))
         quantise(q_codes[1], q_scales[1], q_bf[1][:].rearrange("p q j -> p (q j)"))
@@ -100,6 +101,17 @@ def tile_attend_absorbscores_kernel(tc, query, wuk, lat_words, lat_scales, offs,
                     stop=True,
                 )
             b_ps.append(bank)
+
+        unread = psum.tile([P, C], F32, name="unread")
+        nc.tensor.matmul_mx(
+            out=unread[:],
+            lhsT=q_codes[1][:].bitcast(FP8X4),
+            lhsT_scale=q_scales[1][:],
+            rhs=w_all[:].bitcast(FP8X4),
+            rhs_scale=picked_s[:],
+            start=True,
+            stop=True,
+        )
 
         key_w = []
         b_codes = []

@@ -20,7 +20,7 @@ P = 128
 PACK = 4
 HALF = I // 2
 M_VECTOR = 84
-Q_SCALAR = 48
+Q_SCALAR = 88
 SCALE_ROWS = 16
 
 
@@ -50,28 +50,25 @@ def tile_attend_absorbscores_kernel(tc, query, wuk, lat_words, lat_scales, offs,
         lat_w = keep.tile([P, T], U32, name="lat_w", tag="lat_w", align_bytes=64)
         nc.sync.dma_start(lat_w[:].bitcast(I32), lat_words[0].rearrange("p n t -> p (n t)").bitcast(I32))
 
-        picked_s = keep.tile([P, I], U8, name="picked_s", align_bytes=64)
+        picked_s = reuse.tile([P, I], U8, name="picked_s", align_bytes=64, offset=960)
         nc.vector.tensor_copy(picked_s[:], lat_s[:].indirect(offsets[:]))
         for g in range(4):
             rows = slice(first_row + 4 * g, first_row + 4 * g + 4)
             nc.sync.dma_start(key_s[32 * g : 32 * g + 4, :].bitcast(I32), picked_s[rows, :].bitcast(I32))
 
-        w_bf = reuse.tile([P, PACK, P, PACK], BF16, name="w_bf", align_bytes=64, offset=1024)
+        w_bf = keep.tile([P, PACK, P, PACK], BF16, name="w_bf", align_bytes=64)
         w_src = w_raw[:].rearrange("p j (m t) -> p m t j", t=PACK)
         w_dst = w_bf[:].rearrange("p t m j -> p m t j")
         nc.vector.tensor_copy(w_dst[:, :M_VECTOR], w_src[:, :M_VECTOR])
         nc.scalar.copy(w_dst[:, M_VECTOR:], w_src[:, M_VECTOR:])
-        w_scales = [keep.tile([P, P], U8, name="w_scales%d" % t, align_bytes=64) for t in range(2)]
         w_all = keep.tile([P, C], U32, name="w_all", align_bytes=64)
+        w_plane = keep.tile([P, C], U8, name="w_plane", align_bytes=64)
+        quantise(w_all, w_plane, w_bf[:].rearrange("p t m j -> p (t m j)"))
         w_codes = [w_all[:, t * P : (t + 1) * P] for t in range(PACK)]
-        for t in range(2):
-            quantise(w_codes[t], w_scales[t], w_bf[:, t].rearrange("p m j -> p (m j)"))
+        w_scales = [w_plane[:, t * P : (t + 1) * P] for t in range(PACK)]
 
         q_src = q_raw[:].rearrange("p j (c i) -> p c j i", i=4)
-        q_bf = [
-            reuse.tile([P, P, PACK], BF16, name="q_bf0", align_bytes=64, offset=0),
-            keep.tile([P, P, PACK], BF16, name="q_bf1", align_bytes=64),
-        ]
+        q_bf = [keep.tile([P, P, PACK], BF16, name="q_bf%d" % h, align_bytes=64) for h in range(2)]
         q_dst = [tile[:].rearrange("p (c i) j -> p c j i", i=4) for tile in q_bf]
         cut = Q_SCALAR // 4
         nc.scalar.copy(q_dst[0][:, :cut], q_src[:, :cut])
@@ -80,10 +77,7 @@ def tile_attend_absorbscores_kernel(tc, query, wuk, lat_words, lat_scales, offs,
         q_scales = [keep.tile([P, P], U8, name="q_scales%d" % h, align_bytes=64) for h in range(2)]
         q_codes = [keep.tile([P, P], U32, name="q_codes0", align_bytes=64)]
         quantise(q_codes[0], q_scales[0], q_bf[0][:].rearrange("p q j -> p (q j)"))
-        for t in range(2, PACK):
-            w_scales.append(reuse.tile([P, P], U8, name="w_scales%d" % t, align_bytes=64, offset=512 * (t - 2)))
-            quantise(w_codes[t], w_scales[t], w_bf[:, t].rearrange("p m j -> p (m j)"))
-        q_codes.append(reuse.tile([P, P], U32, name="q_codes1", align_bytes=64, offset=1024))
+        q_codes.append(keep.tile([P, P], U32, name="q_codes1", align_bytes=64))
         quantise(q_codes[1], q_scales[1], q_bf[1][:].rearrange("p q j -> p (q j)"))
 
         halves = [offsets[:, u * (HALF // 16) : (u + 1) * (HALF // 16)] for u in range(2)]
@@ -108,7 +102,7 @@ def tile_attend_absorbscores_kernel(tc, query, wuk, lat_words, lat_scales, offs,
             lhsT=q_codes[1][:].bitcast(FP8X4),
             lhsT_scale=q_scales[1][:],
             rhs=w_all[:].bitcast(FP8X4),
-            rhs_scale=picked_s[:],
+            rhs_scale=w_plane[:],
             start=True,
             stop=True,
         )
@@ -117,28 +111,24 @@ def tile_attend_absorbscores_kernel(tc, query, wuk, lat_words, lat_scales, offs,
         b_codes = []
         b_scales = []
         for h in range(2):
-            if h == 1:
-                for u in range(2):
-                    gathered = keep.tile([P, HALF], U32, name="key_w%d" % u, align_bytes=64)
-                    nc.vector.tensor_copy(gathered[:], lat_w[:].indirect(halves[u]))
-                    key_w.append(gathered)
+            gathered = reuse.tile([P, HALF], U32, name="key_w%d" % h, align_bytes=64, offset=2048 * (1 - h))
+            nc.vector.tensor_copy(gathered[:], lat_w[:].indirect(halves[h]))
+            key_w.append(gathered)
             b_bf = keep.tile([P, P, PACK], BF16, name="b_bf%d" % h, align_bytes=64)
             nc.scalar.copy(b_bf[:], b_ps[h][:].rearrange("p t q -> p q t"))
-            if h == 0:
-                codes = keep.tile([P, P], U32, name="b_codes0", align_bytes=64)
-            else:
-                codes = keep.tile([P, P], U32, name="b_codes1", tag="lat_w", align_bytes=64)
-            scales = keep.tile([P, P], U8, name="b_scales%d" % h, align_bytes=64)
+            codes = keep.tile([P, P], U32, name="b_codes%d" % h, align_bytes=64)
+            scales = reuse.tile([P, P], U8, name="b_scales%d" % h, align_bytes=64, offset=1024 + P * h)
             quantise(codes, scales, b_bf[:].rearrange("p q t -> p (q t)"))
             b_codes.append(codes)
             b_scales.append(scales)
 
-        scores = [psum.tile([P, I], F32, name="scores%d" % h) for h in range(2)]
+        halves_0 = [psum.tile([P, HALF], F32, name="scores0_%d" % u) for u in range(2)]
+        scores_1 = psum.tile([P, I], F32, name="scores1")
         for h in range(2):
             for u in range(2):
                 slots = slice(u * HALF, (u + 1) * HALF)
                 nc.tensor.matmul_mx(
-                    out=scores[h][:, slots],
+                    out=scores_1[:, slots] if h else halves_0[u][:],
                     lhsT=b_codes[h][:].bitcast(FP8X4),
                     lhsT_scale=b_scales[h][:],
                     rhs=key_w[u][:].bitcast(FP8X4),
@@ -149,10 +139,17 @@ def tile_attend_absorbscores_kernel(tc, query, wuk, lat_words, lat_scales, offs,
 
         for h in range(2):
             neg_max = keep.tile([P, 1], F32, name="neg_max%d" % h)
-            nc.vector.tensor_reduce(neg_max[:], scores[h][:], AXIS.X, ALU.max, negate=True)
             p = keep.tile([P, I], F32, name="p%d" % h)
             total = keep.tile([P, 1], F32, name="total%d" % h)
-            nc.scalar.activation(p[:], scores[h][:], ACT.Exp, bias=neg_max[:], scale=1.0, accum_out=total[:])
+            if h == 0:
+                negated = keep.tile([P, I], F32, name="negated")
+                neg_max_a = keep.tile([P, 1], F32, name="neg_max_a")
+                nc.vector.tensor_scalar(negated[:, :HALF], halves_0[0][:], -1.0, None, ALU.mult, ALU.min, accum_out=neg_max_a[:])
+                nc.vector.tensor_scalar(negated[:, HALF:], halves_0[1][:], -1.0, neg_max_a[:], ALU.mult, ALU.min, accum_out=neg_max[:])
+                nc.scalar.activation(p[:], negated[:], ACT.Exp, bias=neg_max[:], scale=-1.0, accum_out=total[:])
+            else:
+                nc.vector.tensor_reduce(neg_max[:], scores_1[:], AXIS.X, ALU.max, negate=True)
+                nc.scalar.activation(p[:], scores_1[:], ACT.Exp, bias=neg_max[:], scale=1.0, accum_out=total[:])
             inv = keep.tile([P, 1], F32, name="inv%d" % h)
             nc.vector.reciprocal(inv[:], total[:])
             rows = slice(h * P, (h + 1) * P)

@@ -19,8 +19,8 @@ AXIS = mybir.AxisListType
 P = 128
 PACK = 4
 HALF = I // 2
-M_VECTOR = 84
-Q_SCALAR = 88
+M_VECTOR = 32
+Q_SCALAR = 96
 SCALE_ROWS = 16
 
 
@@ -56,14 +56,17 @@ def tile_attend_absorbscores_kernel(tc, query, wuk, lat_words, lat_scales, offs,
             rows = slice(first_row + 4 * g, first_row + 4 * g + 4)
             nc.sync.dma_start(key_s[32 * g : 32 * g + 4, :].bitcast(I32), picked_s[rows, :].bitcast(I32))
 
-        w_bf = keep.tile([P, PACK, P, PACK], BF16, name="w_bf", align_bytes=64)
-        w_src = w_raw[:].rearrange("p j (m t) -> p m t j", t=PACK)
-        w_dst = w_bf[:].rearrange("p t m j -> p m t j")
-        nc.vector.tensor_copy(w_dst[:, :M_VECTOR], w_src[:, :M_VECTOR])
-        nc.scalar.copy(w_dst[:, M_VECTOR:], w_src[:, M_VECTOR:])
+        w_src = w_raw[:].rearrange("p j (m t) -> p m j t", t=PACK)
+        w_bf = [keep.tile([P, 2, P, PACK], BF16, name="w_bf%d" % pair, align_bytes=64) for pair in range(2)]
+        w_dst = [tile[:].rearrange("p t m j -> p m j t") for tile in w_bf]
+        nc.vector.tensor_copy(w_dst[0], w_src[:, :, :, :2])
+        nc.vector.tensor_copy(w_dst[1][:, :M_VECTOR], w_src[:, :M_VECTOR, :, 2:])
+        nc.scalar.copy(w_dst[1][:, M_VECTOR:], w_src[:, M_VECTOR:, :, 2:])
         w_all = keep.tile([P, C], U32, name="w_all", align_bytes=64)
         w_plane = keep.tile([P, C], U8, name="w_plane", align_bytes=64)
-        quantise(w_all, w_plane, w_bf[:].rearrange("p t m j -> p (t m j)"))
+        for pair in range(2):
+            cols = slice(pair * 2 * P, (pair + 1) * 2 * P)
+            quantise(w_all[:, cols], w_plane[:, cols], w_bf[pair][:].rearrange("p t m j -> p (t m j)"))
         w_codes = [w_all[:, t * P : (t + 1) * P] for t in range(PACK)]
         w_scales = [w_plane[:, t * P : (t + 1) * P] for t in range(PACK)]
 

@@ -156,7 +156,7 @@ def tile_attend_absorbscores_kernel(tc, query, wuk, lat_words, lat_scales, offs,
             inv = keep.tile([P, 1], F32, name="inv%d" % h)
             nc.vector.reciprocal(inv[:], total[:])
             rows = slice(h * P, (h + 1) * P)
-            pieces = 1 + h
+            pieces = 1
             width = I // pieces
             for v in range(pieces):
                 part = slice(v * width, (v + 1) * width)

@@ -35,19 +35,19 @@ def tile_attend_absorbscores_kernel(tc, query, wuk, lat_words, lat_scales, offs,
             nc.vector.quantize_mx(out=codes[:].bitcast(FP8X4), scales=scales[:], in_=values)
 
         first_row = P - SCALE_ROWS
-        lat_s = keep.tile([P, T], U8, name="lat_s", align_bytes=64)
+        lat_s = keep.tile([P, T], U8, name="lat_s", align_bytes=256)
         nc.scalar.dma_start(lat_s[first_row:, :].bitcast(I32), lat_scales[0].bitcast(I32))
         nc.vector.memset(lat_s[:first_row, :].bitcast(I32), 0)
-        key_s = keep.tile([P, I], U8, name="key_s", align_bytes=64)
+        key_s = keep.tile([P, I], U8, name="key_s", align_bytes=256)
         nc.vector.memset(key_s[:].bitcast(I32), 0)
 
         offsets = keep.tile([P, I // 16], U16, name="offsets")
         nc.sync.dma_start(offsets[:], offs)
-        w_raw = keep.tile([P, PACK, C], F32, name="w_raw")
+        w_raw = keep.tile([P, PACK, C], F32, name="w_raw", align_bytes=256)
         nc.sync.dma_start(w_raw[:], wuk.rearrange("(p j) c -> p j c", j=PACK))
-        q_raw = keep.tile([P, PACK, Q], F32, name="q_raw")
+        q_raw = keep.tile([P, PACK, Q], F32, name="q_raw", align_bytes=256)
         nc.sync.dma_start(q_raw[:], query.rearrange("(p j) q -> p j q", j=PACK))
-        lat_w = keep.tile([P, T], U32, name="lat_w", tag="lat_w", align_bytes=64)
+        lat_w = keep.tile([P, T], U32, name="lat_w", tag="lat_w", align_bytes=256)
         nc.sync.dma_start(lat_w[:].bitcast(I32), lat_words[0].rearrange("p n t -> p (n t)").bitcast(I32))
 
         picked_s = reuse.tile([P, I], U8, name="picked_s", align_bytes=64, offset=960)
@@ -160,7 +160,7 @@ def tile_attend_absorbscores_kernel(tc, query, wuk, lat_words, lat_scales, offs,
             width = I // pieces
             for v in range(pieces):
                 part = slice(v * width, (v + 1) * width)
-                y = keep.tile([P, width], F32, name="y%d_%d" % (h, v))
+                y = keep.tile([P, width], F32, name="y%d_%d" % (h, v), align_bytes=256)
                 nc.vector.tensor_scalar(y[:], p[:, part], inv[:], 512.0, ALU.mult, ALU.mult)
                 queue = nc.scalar if v else nc.sync
                 queue.dma_start(out[rows, part], y[:])

@@ -118,7 +118,7 @@ def tile_attend_absorbscores_kernel(tc, query, wuk, lat_words, lat_scales, offs,
             nc.vector.tensor_copy(gathered[:], lat_w[:].indirect(halves[h]))
             key_w.append(gathered)
             b_bf = keep.tile([P, P, PACK], BF16, name="b_bf%d" % h, align_bytes=64)
-            nc.scalar.copy(b_bf[:], b_ps[h][:].rearrange("p t q -> p q t"))
+            nc.scalar.copy(b_bf[:].rearrange("p (a r) t -> p a r t", r=PACK), b_ps[h][:].rearrange("p t (r a) -> p a r t", r=PACK))
             codes = keep.tile([P, P], U32, name="b_codes%d" % h, align_bytes=64)
             scales = reuse.tile([P, P], U8, name="b_scales%d" % h, align_bytes=64, offset=1024 + P * h)
             quantise(codes, scales, b_bf[:].rearrange("p q t -> p (q t)"))
@@ -163,4 +163,4 @@ def tile_attend_absorbscores_kernel(tc, query, wuk, lat_words, lat_scales, offs,
                 y = keep.tile([P, width], F32, name="y%d_%d" % (h, v), align_bytes=256)
                 nc.vector.tensor_scalar(y[:], p[:, part], inv[:], 512.0, ALU.mult, ALU.mult)
                 queue = nc.scalar if v else nc.sync
-                queue.dma_start(out[rows, part], y[:])
+                queue.dma_start(out[rows, part].rearrange("(r a) i -> a r i", r=PACK), y[:])

@@ -52,9 +52,10 @@ def tile_attend_absorbscores_kernel(tc, query, wuk, lat_words, lat_scales, offs,
 
         picked_s = reuse.tile([P, I], U8, name="picked_s", align_bytes=64, offset=960)
         nc.vector.tensor_copy(picked_s[:], lat_s[:].indirect(offsets[:]))
-        for g in range(4):
+        first, second, both = slice(0, HALF), slice(HALF, I), slice(0, I)
+        for g, slots in ((0, first), (1, first), (2, both), (3, both), (0, second), (1, second)):
             rows = slice(first_row + 4 * g, first_row + 4 * g + 4)
-            nc.sync.dma_start(key_s[32 * g : 32 * g + 4, :].bitcast(I32), picked_s[rows, :].bitcast(I32))
+            nc.sync.dma_start(key_s[32 * g : 32 * g + 4, slots].bitcast(I32), picked_s[rows, slots].bitcast(I32))
 
         w_src = w_raw[:].rearrange("p j (m t) -> p m j t", t=PACK)
         w_bf = [keep.tile([P, 2, P, PACK], BF16, name="w_bf%d" % pair, align_bytes=64) for pair in range(2)]

@@ -152,8 +152,9 @@ def tile_attend_absorbscores_kernel(tc, query, wuk, lat_words, lat_scales, offs,
                 nc.vector.tensor_scalar(negated[:, HALF:], halves_0[1][:], -1.0, neg_max_a[:], ALU.mult, ALU.min, accum_out=neg_max[:])
                 nc.scalar.activation(p[:], negated[:], ACT.Exp, bias=neg_max[:], scale=-1.0, accum_out=total[:])
             else:
-                nc.vector.tensor_reduce(neg_max[:], scores_1[:], AXIS.X, ALU.max, negate=True)
-                nc.scalar.activation(p[:], scores_1[:], ACT.Exp, bias=neg_max[:], scale=1.0, accum_out=total[:])
+                negated = keep.tile([P, I], F32, name="negated1")
+                nc.vector.tensor_scalar(negated[:], scores_1[:], -1.0, None, ALU.mult, ALU.min, accum_out=neg_max[:])
+                nc.scalar.activation(p[:], negated[:], ACT.Exp, bias=neg_max[:], scale=-1.0, accum_out=total[:])
             inv = keep.tile([P, 1], F32, name="inv%d" % h)
             nc.vector.reciprocal(inv[:], total[:])
             rows = slice(h * P, (h + 1) * P)

@@ -22,6 +22,9 @@ HALF = I // 2
 M_VECTOR = 32
 Q_SCALAR = 96
 SCALE_ROWS = 16
+WARM_M = 32
+WARM_AHEAD = 4
+WARM_BEHIND = 2
 
 
 def tile_attend_absorbscores_kernel(tc, query, wuk, lat_words, lat_scales, offs, out):
@@ -33,6 +36,19 @@ def tile_attend_absorbscores_kernel(tc, query, wuk, lat_words, lat_scales, offs,
 
         def quantise(codes, scales, values):
             nc.vector.quantize_mx(out=codes[:].bitcast(FP8X4), scales=scales[:], in_=values)
+
+        def warm_up(codes, scales, passes):
+            unread = psum.tile([WARM_M, passes, P], F32, name="unread%d" % passes)
+            for k in range(passes):
+                nc.tensor.matmul_mx(
+                    out=unread[:, k, :],
+                    lhsT=codes[:, :WARM_M].bitcast(FP8X4),
+                    lhsT_scale=scales[:, :WARM_M],
+                    rhs=w_all[:, :P].bitcast(FP8X4),
+                    rhs_scale=w_plane[:, :P],
+                    start=True,
+                    stop=True,
+                )
 
         first_row = P - SCALE_ROWS
         lat_s = keep.tile([P, T], U8, name="lat_s", align_bytes=256)
@@ -71,6 +87,8 @@ def tile_attend_absorbscores_kernel(tc, query, wuk, lat_words, lat_scales, offs,
         w_codes = [w_all[:, t * P : (t + 1) * P] for t in range(PACK)]
         w_scales = [w_plane[:, t * P : (t + 1) * P] for t in range(PACK)]
 
+        warm_up(w_all, w_plane, WARM_AHEAD)
+
         q_src = q_raw[:].rearrange("p j (c i) -> p c j i", i=4)
         q_bf = [keep.tile([P, P, PACK], BF16, name="q_bf%d" % h, align_bytes=64) for h in range(2)]
         q_dst = [tile[:].rearrange("p (c i) j -> p c j i", i=4) for tile in q_bf]
@@ -100,16 +118,7 @@ def tile_attend_absorbscores_kernel(tc, query, wuk, lat_words, lat_scales, offs,
                 )
             b_ps.append(bank)
 
-        unread = psum.tile([P, C], F32, name="unread")
-        nc.tensor.matmul_mx(
-            out=unread[:],
-            lhsT=q_codes[1][:].bitcast(FP8X4),
-            lhsT_scale=q_scales[1][:],
-            rhs=w_all[:].bitcast(FP8X4),
-            rhs_scale=w_plane[:],
-            start=True,
-            stop=True,
-        )
+        warm_up(q_codes[1], q_scales[1], WARM_BEHIND)
 
         key_w = []
         b_codes = []

@@ -14,17 +14,21 @@ U8 = mybir.dt.uint8
 FP8X4 = mybir.dt.float8_e4m3fn_x4
 ALU = mybir.AluOpType
 ACT = mybir.ActivationFunctionType
-AXIS = mybir.AxisListType
 
 P = 128
 PACK = 4
 HALF = I // 2
-M_VECTOR = 32
-Q_SCALAR = 96
 SCALE_ROWS = 16
 WARM_M = 32
 WARM_AHEAD = 4
 WARM_BEHIND = 2
+Q_SCALAR = 32
+HEAD = 256
+REST_AT = 1024 - 4 * (I - HEAD) if HEAD >= HALF else 1408
+GATHERS = ((256, 384), (384, 512))
+SPLIT = 256
+PASSES_0 = ((0, 256), (256, 384), (384, 512))
+PASSES_1 = ((0, 256), (256, 512))
 
 
 def tile_attend_absorbscores_kernel(tc, query, wuk, lat_words, lat_scales, offs, out):
@@ -35,20 +39,23 @@ def tile_attend_absorbscores_kernel(tc, query, wuk, lat_words, lat_scales, offs,
         psum = ctx.enter_context(tc.psum_pool(name="psum", bufs=1))
 
         def quantise(codes, scales, values):
-            nc.vector.quantize_mx(out=codes[:].bitcast(FP8X4), scales=scales[:], in_=values)
+            nc.vector.quantize_mx(out=codes.bitcast(FP8X4), scales=scales, in_=values)
+
+        def product(result, stationary, stationary_scales, moving, moving_scales):
+            nc.tensor.matmul_mx(
+                out=result,
+                lhsT=stationary.bitcast(FP8X4),
+                lhsT_scale=stationary_scales,
+                rhs=moving.bitcast(FP8X4),
+                rhs_scale=moving_scales,
+                start=True,
+                stop=True,
+            )
 
         def warm_up(codes, scales, passes):
             unread = psum.tile([WARM_M, passes, P], F32, name="unread%d" % passes)
             for k in range(passes):
-                nc.tensor.matmul_mx(
-                    out=unread[:, k, :],
-                    lhsT=codes[:, :WARM_M].bitcast(FP8X4),
-                    lhsT_scale=scales[:, :WARM_M],
-                    rhs=w_all[:, :P].bitcast(FP8X4),
-                    rhs_scale=w_plane[:, :P],
-                    start=True,
-                    stop=True,
-                )
+                product(unread[:, k, :], codes[:, :WARM_M], scales[:, :WARM_M], w_codes[:, :P], w_scales[:, :P])
 
         first_row = P - SCALE_ROWS
         lat_s = keep.tile([P, T], U8, name="lat_s", align_bytes=256)
@@ -63,7 +70,7 @@ def tile_attend_absorbscores_kernel(tc, query, wuk, lat_words, lat_scales, offs,
         nc.sync.dma_start(w_raw[:], wuk.rearrange("(p j) c -> p j c", j=PACK))
         q_raw = keep.tile([P, PACK, Q], F32, name="q_raw", align_bytes=256)
         nc.sync.dma_start(q_raw[:], query.rearrange("(p j) q -> p j q", j=PACK))
-        lat_w = keep.tile([P, T], U32, name="lat_w", tag="lat_w", align_bytes=256)
+        lat_w = keep.tile([P, T], U32, name="lat_w", align_bytes=256)
         nc.sync.dma_start(lat_w[:].bitcast(I32), lat_words[0].rearrange("p n t -> p (n t)").bitcast(I32))
 
         picked_s = reuse.tile([P, I], U8, name="picked_s", align_bytes=64, offset=960)
@@ -77,101 +84,84 @@ def tile_attend_absorbscores_kernel(tc, query, wuk, lat_words, lat_scales, offs,
         w_bf = [keep.tile([P, 2, P, PACK], BF16, name="w_bf%d" % pair, align_bytes=64) for pair in range(2)]
         w_dst = [tile[:].rearrange("p t m j -> p m j t") for tile in w_bf]
         nc.vector.tensor_copy(w_dst[0], w_src[:, :, :, :2])
-        nc.vector.tensor_copy(w_dst[1][:, :M_VECTOR], w_src[:, :M_VECTOR, :, 2:])
-        nc.scalar.copy(w_dst[1][:, M_VECTOR:], w_src[:, M_VECTOR:, :, 2:])
-        w_all = keep.tile([P, C], U32, name="w_all", align_bytes=64)
-        w_plane = keep.tile([P, C], U8, name="w_plane", align_bytes=64)
-        for pair in range(2):
-            cols = slice(pair * 2 * P, (pair + 1) * 2 * P)
-            quantise(w_all[:, cols], w_plane[:, cols], w_bf[pair][:].rearrange("p t m j -> p (t m j)"))
-        w_codes = [w_all[:, t * P : (t + 1) * P] for t in range(PACK)]
-        w_scales = [w_plane[:, t * P : (t + 1) * P] for t in range(PACK)]
+        nc.scalar.copy(w_dst[1], w_src[:, :, :, 2:])
+        w_codes = keep.tile([P, C], U32, name="w_codes", align_bytes=64)
+        w_scales = keep.tile([P, C], U8, name="w_scales", align_bytes=64)
 
-        warm_up(w_all, w_plane, WARM_AHEAD)
+        def quantise_pair(pair):
+            cols = slice(pair * 2 * P, (pair + 1) * 2 * P)
+            quantise(w_codes[:, cols], w_scales[:, cols], w_bf[pair][:].rearrange("p t m j -> p (t m j)"))
+
+        quantise_pair(0)
+        warm_up(w_codes, w_scales, WARM_AHEAD)
 
         q_src = q_raw[:].rearrange("p j (c i) -> p c j i", i=4)
         q_bf = [keep.tile([P, P, PACK], BF16, name="q_bf%d" % h, align_bytes=64) for h in range(2)]
         q_dst = [tile[:].rearrange("p (c i) j -> p c j i", i=4) for tile in q_bf]
         cut = Q_SCALAR // 4
-        nc.scalar.copy(q_dst[0][:, :cut], q_src[:, :cut])
         nc.vector.tensor_copy(q_dst[0][:, cut:], q_src[:, cut : P // 4])
+        nc.scalar.copy(q_dst[0][:, :cut], q_src[:, :cut])
         nc.scalar.copy(q_dst[1], q_src[:, P // 4 :])
+        quantise_pair(1)
         q_scales = [keep.tile([P, P], U8, name="q_scales%d" % h, align_bytes=64) for h in range(2)]
-        q_codes = [keep.tile([P, P], U32, name="q_codes0", align_bytes=64)]
-        quantise(q_codes[0], q_scales[0], q_bf[0][:].rearrange("p q j -> p (q j)"))
-        q_codes.append(keep.tile([P, P], U32, name="q_codes1", align_bytes=64))
-        quantise(q_codes[1], q_scales[1], q_bf[1][:].rearrange("p q j -> p (q j)"))
-
-        halves = [offsets[:, u * (HALF // 16) : (u + 1) * (HALF // 16)] for u in range(2)]
-        b_ps = []
+        q_codes = [keep.tile([P, P], U32, name="q_codes%d" % h, align_bytes=64) for h in range(2)]
         for h in range(2):
-            bank = psum.tile([P, PACK, P], F32, name="b_ps%d" % h)
-            for t in range(PACK):
-                nc.tensor.matmul_mx(
-                    out=bank[:, t, :],
-                    lhsT=w_codes[t][:].bitcast(FP8X4),
-                    lhsT_scale=w_scales[t][:],
-                    rhs=q_codes[h][:].bitcast(FP8X4),
-                    rhs_scale=q_scales[h][:],
-                    start=True,
-                    stop=True,
-                )
-            b_ps.append(bank)
+            quantise(q_codes[h][:], q_scales[h][:], q_bf[h][:].rearrange("p q j -> p (q j)"))
 
+        b_ps = [psum.tile([P, PACK, P], F32, name="b_ps%d" % h) for h in range(2)]
+        for h in range(2):
+            for t in range(PACK):
+                cols = slice(t * P, (t + 1) * P)
+                product(b_ps[h][:, t, :], w_codes[:, cols], w_scales[:, cols], q_codes[h][:], q_scales[h][:])
         warm_up(q_codes[1], q_scales[1], WARM_BEHIND)
 
-        key_w = []
-        b_codes = []
-        b_scales = []
+        b_bf = [keep.tile([P, P, PACK], BF16, name="b_bf%d" % h, align_bytes=64) for h in range(2)]
+        b_codes = [keep.tile([P, P], U32, name="b_codes%d" % h, align_bytes=64) for h in range(2)]
+        b_scales = [reuse.tile([P, P], U8, name="b_scales%d" % h, align_bytes=64, offset=1024 + P * h) for h in range(2)]
         for h in range(2):
-            gathered = reuse.tile([P, HALF], U32, name="key_w%d" % h, align_bytes=64, offset=2048 * (1 - h))
-            nc.vector.tensor_copy(gathered[:], lat_w[:].indirect(halves[h]))
-            key_w.append(gathered)
-            b_bf = keep.tile([P, P, PACK], BF16, name="b_bf%d" % h, align_bytes=64)
-            nc.scalar.copy(b_bf[:].rearrange("p (a r) t -> p a r t", r=PACK), b_ps[h][:].rearrange("p t (r a) -> p a r t", r=PACK))
-            codes = keep.tile([P, P], U32, name="b_codes%d" % h, align_bytes=64)
-            scales = reuse.tile([P, P], U8, name="b_scales%d" % h, align_bytes=64, offset=1024 + P * h)
-            quantise(codes, scales, b_bf[:].rearrange("p q t -> p (q t)"))
-            b_codes.append(codes)
-            b_scales.append(scales)
+            nc.scalar.copy(b_bf[h][:].rearrange("p (a r) t -> p a r t", r=PACK), b_ps[h][:].rearrange("p t (r a) -> p a r t", r=PACK))
 
-        halves_0 = [psum.tile([P, HALF], F32, name="scores0_%d" % u) for u in range(2)]
+        head = keep.tile([P, HEAD], U32, name="key_head", align_bytes=64)
+        rest = reuse.tile([P, I - HEAD], U32, name="key_rest", align_bytes=64, offset=REST_AT)
+
+        def keys(a, b):
+            return head[:, a:b] if b <= HEAD else rest[:, a - HEAD : b - HEAD]
+
+        def gather(a, b):
+            nc.vector.tensor_copy(keys(a, b), lat_w[:].indirect(offsets[:, a // 16 : b // 16]))
+
+        def quantise_b(h):
+            quantise(b_codes[h][:], b_scales[h][:], b_bf[h][:].rearrange("p q t -> p (q t)"))
+
+        gather(0, HEAD)
+        quantise_b(0)
+        for a, b in GATHERS:
+            gather(a, b)
+        quantise_b(1)
+
+        early = psum.tile([P, SPLIT], F32, name="scores0_early")
+        late = psum.tile([P, I - SPLIT], F32, name="scores0_late")
         scores_1 = psum.tile([P, I], F32, name="scores1")
-        for h in range(2):
-            for u in range(2):
-                slots = slice(u * HALF, (u + 1) * HALF)
-                nc.tensor.matmul_mx(
-                    out=scores_1[:, slots] if h else halves_0[u][:],
-                    lhsT=b_codes[h][:].bitcast(FP8X4),
-                    lhsT_scale=b_scales[h][:],
-                    rhs=key_w[u][:].bitcast(FP8X4),
-                    rhs_scale=key_s[:, slots],
-                    start=True,
-                    stop=True,
-                )
+        for a, b in PASSES_0:
+            result = early[:, a:b] if b <= SPLIT else late[:, a - SPLIT : b - SPLIT]
+            product(result, b_codes[0][:], b_scales[0][:], keys(a, b), key_s[:, a:b])
+        for a, b in PASSES_1:
+            product(scores_1[:, a:b], b_codes[1][:], b_scales[1][:], keys(a, b), key_s[:, a:b])
 
         for h in range(2):
             neg_max = keep.tile([P, 1], F32, name="neg_max%d" % h)
+            negated = keep.tile([P, I], F32, name="negated%d" % h)
             p = keep.tile([P, I], F32, name="p%d" % h)
             total = keep.tile([P, 1], F32, name="total%d" % h)
             if h == 0:
-                negated = keep.tile([P, I], F32, name="negated")
-                neg_max_a = keep.tile([P, 1], F32, name="neg_max_a")
-                nc.vector.tensor_scalar(negated[:, :HALF], halves_0[0][:], -1.0, None, ALU.mult, ALU.min, accum_out=neg_max_a[:])
-                nc.vector.tensor_scalar(negated[:, HALF:], halves_0[1][:], -1.0, neg_max_a[:], ALU.mult, ALU.min, accum_out=neg_max[:])
-                nc.scalar.activation(p[:], negated[:], ACT.Exp, bias=neg_max[:], scale=-1.0, accum_out=total[:])
+                neg_max_early = keep.tile([P, 1], F32, name="neg_max_early")
+                nc.vector.tensor_scalar(negated[:, :SPLIT], early[:], -1.0, None, ALU.mult, ALU.min, accum_out=neg_max_early[:])
+                nc.vector.tensor_scalar(negated[:, SPLIT:], late[:], -1.0, neg_max_early[:], ALU.mult, ALU.min, accum_out=neg_max[:])
             else:
-                negated = keep.tile([P, I], F32, name="negated1")
                 nc.vector.tensor_scalar(negated[:], scores_1[:], -1.0, None, ALU.mult, ALU.min, accum_out=neg_max[:])
-                nc.scalar.activation(p[:], negated[:], ACT.Exp, bias=neg_max[:], scale=-1.0, accum_out=total[:])
+            nc.scalar.activation(p[:], negated[:], ACT.Exp, bias=neg_max[:], scale=-1.0, accum_out=total[:])
             inv = keep.tile([P, 1], F32, name="inv%d" % h)
             nc.vector.reciprocal(inv[:], total[:])
-            rows = slice(h * P, (h + 1) * P)
-            pieces = 1
-            width = I // pieces
-            for v in range(pieces):
-                part = slice(v * width, (v + 1) * width)
-                y = keep.tile([P, width], F32, name="y%d_%d" % (h, v), align_bytes=256)
-                nc.vector.tensor_scalar(y[:], p[:, part], inv[:], 512.0, ALU.mult, ALU.mult)
-                queue = nc.scalar if v else nc.sync
-                queue.dma_start(out[rows, part].rearrange("(r a) i -> a r i", r=PACK), y[:])
+            y = keep.tile([P, I], F32, name="y%d" % h, align_bytes=256)
+            nc.vector.tensor_scalar(y[:], p[:], inv[:], 512.0, ALU.mult, ALU.mult)
+            nc.sync.dma_start(out[h * P : (h + 1) * P, :].rearrange("(r a) i -> a r i", r=PACK), y[:])

@@ -25,9 +25,9 @@ WARM_BEHIND = 2
 Q_SCALAR = 32
 HEAD = 256
 REST_AT = 1024 - 4 * (I - HEAD) if HEAD >= HALF else 1408
-GATHERS = ((256, 384), (384, 512))
+GATHERS = ((256, 512),)
 SPLIT = 256
-PASSES_0 = ((0, 256), (256, 384), (384, 512))
+PASSES_0 = ((0, 256), (256, 512))
 PASSES_1 = ((0, 256), (256, 512))
 
 

@@ -67,11 +67,11 @@ def tile_attend_absorbscores_kernel(tc, query, wuk, lat_words, lat_scales, offs,
         offsets = keep.tile([P, I // 16], U16, name="offsets")
         nc.sync.dma_start(offsets[:], offs)
         w_raw = keep.tile([P, PACK, C], F32, name="w_raw", align_bytes=256)
-        nc.sync.dma_start(w_raw[:], wuk.rearrange("(p j) c -> p j c", j=PACK))
+        nc.sync.dma_start(w_raw[:], wuk.rearrange("(p j) c -> p j c", j=PACK), max_dma_last_dim=4096)
         q_raw = keep.tile([P, PACK, Q], F32, name="q_raw", align_bytes=256)
         nc.sync.dma_start(q_raw[:], query.rearrange("(p j) q -> p j q", j=PACK))
         lat_w = keep.tile([P, T], U32, name="lat_w", align_bytes=256)
-        nc.sync.dma_start(lat_w[:].bitcast(I32), lat_words[0].rearrange("p n t -> p (n t)").bitcast(I32))
+        nc.sync.dma_start(lat_w[:].bitcast(I32), lat_words[0].rearrange("p n t -> p (n t)").bitcast(I32), max_dma_last_dim=4096)
 
         picked_s = reuse.tile([P, I], U8, name="picked_s", align_bytes=64, offset=960)
         nc.vector.tensor_copy(picked_s[:], lat_s[:].indirect(offsets[:]))

@@ -70,15 +70,20 @@ def tile_attend_absorbscores_kernel(tc, query, wuk, lat_words, lat_scales, offs,
         nc.sync.dma_start(w_raw[:], wuk.rearrange("(p j) c -> p j c", j=PACK), max_dma_last_dim=4096)
         q_raw = keep.tile([P, PACK, Q], F32, name="q_raw", align_bytes=256)
         nc.sync.dma_start(q_raw[:], query.rearrange("(p j) q -> p j q", j=PACK))
-        lat_w = keep.tile([P, T], U32, name="lat_w", align_bytes=256)
-        nc.sync.dma_start(lat_w[:].bitcast(I32), lat_words[0].rearrange("p n t -> p (n t)").bitcast(I32), max_dma_last_dim=4096)
 
         picked_s = reuse.tile([P, I], U8, name="picked_s", align_bytes=64, offset=960)
-        nc.vector.tensor_copy(picked_s[:], lat_s[:].indirect(offsets[:]))
-        first, second, both = slice(0, HALF), slice(HALF, I), slice(0, I)
-        for g, slots in ((0, first), (1, first), (2, both), (3, both), (0, second), (1, second)):
+        for a in (0, HALF):
+            nc.vector.tensor_copy(picked_s[:, a : a + HALF], lat_s[:].indirect(offsets[:, a // 16 : (a + HALF) // 16]))
+        first, second = slice(0, HALF), slice(HALF, I)
+        def move(g, slots):
             rows = slice(first_row + 4 * g, first_row + 4 * g + 4)
             nc.sync.dma_start(key_s[32 * g : 32 * g + 4, slots].bitcast(I32), picked_s[rows, slots].bitcast(I32))
+
+        move(0, first)
+        lat_w = keep.tile([P, T], U32, name="lat_w", align_bytes=256)
+        nc.sync.dma_start(lat_w[:].bitcast(I32), lat_words[0].rearrange("p n t -> p (n t)").bitcast(I32), max_dma_last_dim=4096)
+        for g, slots in ((1, first), (2, first), (3, first), (0, second), (1, second), (2, second), (3, second)):
+            move(g, slots)
 
         w_src = w_raw[:].rearrange("p j (m t) -> p m j t", t=PACK)
         w_bf = [keep.tile([P, 2, P, PACK], BF16, name="w_bf%d" % pair, align_bytes=64) for pair in range(2)]

@@ -23,6 +23,7 @@ WARM_M = 32
 WARM_AHEAD = 4
 WARM_BEHIND = 2
 Q_SCALAR = 32
+MOVES_AHEAD = 3
 HEAD = 256
 REST_AT = 1024 - 4 * (I - HEAD) if HEAD >= HALF else 1408
 GATHERS = ((256, 512),)
@@ -79,11 +80,14 @@ def tile_attend_absorbscores_kernel(tc, query, wuk, lat_words, lat_scales, offs,
             rows = slice(first_row + 4 * g, first_row + 4 * g + 4)
             nc.sync.dma_start(key_s[32 * g : 32 * g + 4, slots].bitcast(I32), picked_s[rows, slots].bitcast(I32))
 
-        move(0, first)
+        for g in range(MOVES_AHEAD):
+            move(g, first)
         lat_w = keep.tile([P, T], U32, name="lat_w", align_bytes=256)
         nc.sync.dma_start(lat_w[:].bitcast(I32), lat_words[0].rearrange("p n t -> p (n t)").bitcast(I32), max_dma_last_dim=4096)
-        for g, slots in ((1, first), (2, first), (3, first), (0, second), (1, second), (2, second), (3, second)):
-            move(g, slots)
+        for g in range(MOVES_AHEAD, 4):
+            move(g, first)
+        for g in range(4):
+            move(g, second)
 
         w_src = w_raw[:].rearrange("p j (m t) -> p m j t", t=PACK)
         w_bf = [keep.tile([P, 2, P, PACK], BF16, name="w_bf%d" % pair, align_bytes=64) for pair in range(2)]

@@ -23,6 +23,7 @@ WARM_M = 32
 WARM_AHEAD = 4
 WARM_BEHIND = 2
 Q_SCALAR = 32
+MOVE_CUT = 128
 MOVES_AHEAD = 3
 HEAD = 256
 REST_AT = 1024 - 4 * (I - HEAD) if HEAD >= HALF else 1408
@@ -75,7 +76,7 @@ def tile_attend_absorbscores_kernel(tc, query, wuk, lat_words, lat_scales, offs,
         picked_s = reuse.tile([P, I], U8, name="picked_s", align_bytes=64, offset=960)
         for a in (0, HALF):
             nc.vector.tensor_copy(picked_s[:, a : a + HALF], lat_s[:].indirect(offsets[:, a // 16 : (a + HALF) // 16]))
-        first, second = slice(0, HALF), slice(HALF, I)
+        first, second = slice(0, MOVE_CUT), slice(MOVE_CUT, I)
         def move(g, slots):
             rows = slice(first_row + 4 * g, first_row + 4 * g + 4)
             nc.sync.dma_start(key_s[32 * g : 32 * g + 4, slots].bitcast(I32), picked_s[rows, slots].bitcast(I32))

@@ -73,7 +73,7 @@ def tile_attend_absorbscores_kernel(tc, query, wuk, lat_words, lat_scales, offs,
         q_raw = keep.tile([P, PACK, Q], F32, name="q_raw", align_bytes=256)
         nc.sync.dma_start(q_raw[:], query.rearrange("(p j) q -> p j q", j=PACK))
 
-        picked_s = reuse.tile([P, I], U8, name="picked_s", align_bytes=64, offset=960)
+        picked_s = keep.tile([P, I], U8, name="picked_s", align_bytes=64)
         for a in (0, HALF):
             nc.vector.tensor_copy(picked_s[:, a : a + HALF], lat_s[:].indirect(offsets[:, a // 16 : (a + HALF) // 16]))
         first, second = slice(0, MOVE_CUT), slice(MOVE_CUT, I)
@@ -87,8 +87,11 @@ def tile_attend_absorbscores_kernel(tc, query, wuk, lat_words, lat_scales, offs,
         nc.sync.dma_start(lat_w[:].bitcast(I32), lat_words[0].rearrange("p n t -> p (n t)").bitcast(I32), max_dma_last_dim=4096)
         for g in range(MOVES_AHEAD, 4):
             move(g, first)
-        for g in range(4):
+        for g in range(3):
             move(g, second)
+        picked_last = reuse.tile([P, I - MOVE_CUT], U8, name="picked_last", align_bytes=64, offset=960)
+        nc.vector.tensor_copy(picked_last[:].bitcast(I32), picked_s[:, second].bitcast(I32))
+        nc.sync.dma_start(key_s[96:100, second].bitcast(I32), picked_last[first_row + 12 :, :].bitcast(I32))
 
         w_src = w_raw[:].rearrange("p j (m t) -> p m j t", t=PACK)
         w_bf = [keep.tile([P, 2, P, PACK], BF16, name="w_bf%d" % pair, align_bytes=64) for pair in range(2)]

from contextlib import ExitStack

import concourse.mybir as mybir

D, C, T, I, Q = 512, 512, 2048, 512, 256
FLOPS = 2 * D * C * Q + 2 * C * Q * I

F32 = mybir.dt.float32
BF16 = mybir.dt.bfloat16
I32 = mybir.dt.int32
U32 = mybir.dt.uint32
U16 = mybir.dt.uint16
U8 = mybir.dt.uint8
FP8X4 = mybir.dt.float8_e4m3fn_x4
ALU = mybir.AluOpType
ACT = mybir.ActivationFunctionType

P = 128
PACK = 4
HALF = I // 2
SCALE_ROWS = 16
WARM_M = 32
WARM_AHEAD = 4
WARM_BEHIND = 2
Q_SCALAR = 32
MOVE_CUT = 128
MOVES_AHEAD = 3
HEAD = 256
REST_AT = 1024 - 4 * (I - HEAD) if HEAD >= HALF else 1408
GATHERS = ((256, 512),)
SPLIT = 256
PASSES_0 = ((0, 256), (256, 512))
PASSES_1 = ((0, 256), (256, 512))


def tile_attend_absorbscores_kernel(tc, query, wuk, lat_words, lat_scales, offs, out):
    nc = tc.nc
    with ExitStack() as ctx:
        keep = ctx.enter_context(tc.tile_pool(name="keep", bufs=1))
        reuse = ctx.enter_context(tc.tile_pool(name="reuse", bufs=1))
        psum = ctx.enter_context(tc.psum_pool(name="psum", bufs=1))

        def quantise(codes, scales, values):
            nc.vector.quantize_mx(out=codes.bitcast(FP8X4), scales=scales, in_=values)

        def product(result, stationary, stationary_scales, moving, moving_scales):
            nc.tensor.matmul_mx(
                out=result,
                lhsT=stationary.bitcast(FP8X4),
                lhsT_scale=stationary_scales,
                rhs=moving.bitcast(FP8X4),
                rhs_scale=moving_scales,
                start=True,
                stop=True,
            )

        def warm_up(codes, scales, passes):
            unread = psum.tile([WARM_M, passes, P], F32, name="unread%d" % passes)
            for k in range(passes):
                product(unread[:, k, :], codes[:, :WARM_M], scales[:, :WARM_M], w_codes[:, :P], w_scales[:, :P])

        first_row = P - SCALE_ROWS
        lat_s = keep.tile([P, T], U8, name="lat_s", align_bytes=256)
        nc.scalar.dma_start(lat_s[first_row:, :].bitcast(I32), lat_scales[0].bitcast(I32))
        nc.vector.memset(lat_s[:first_row, :].bitcast(I32), 0)
        key_s = keep.tile([P, I], U8, name="key_s", align_bytes=256)
        nc.vector.memset(key_s[:].bitcast(I32), 0)

        offsets = keep.tile([P, I // 16], U16, name="offsets")
        nc.sync.dma_start(offsets[:], offs)
        w_raw = keep.tile([P, PACK, C], F32, name="w_raw", align_bytes=256)
        nc.sync.dma_start(w_raw[:], wuk.rearrange("(p j) c -> p j c", j=PACK), max_dma_last_dim=4096)
        q_raw = keep.tile([P, PACK, Q], F32, name="q_raw", align_bytes=256)
        nc.sync.dma_start(q_raw[:], query.rearrange("(p j) q -> p j q", j=PACK))

        picked_s = keep.tile([P, I], U8, name="picked_s", align_bytes=64)
        for a in (0, HALF):
            nc.vector.tensor_copy(picked_s[:, a : a + HALF], lat_s[:].indirect(offsets[:, a // 16 : (a + HALF) // 16]))
        first, second = slice(0, MOVE_CUT), slice(MOVE_CUT, I)
        def move(g, slots):
            rows = slice(first_row + 4 * g, first_row + 4 * g + 4)
            nc.sync.dma_start(key_s[32 * g : 32 * g + 4, slots].bitcast(I32), picked_s[rows, slots].bitcast(I32))

        for g in range(MOVES_AHEAD):
            move(g, first)
        lat_w = keep.tile([P, T], U32, name="lat_w", align_bytes=256)
        nc.sync.dma_start(lat_w[:].bitcast(I32), lat_words[0].rearrange("p n t -> p (n t)").bitcast(I32), max_dma_last_dim=4096)
        for g in range(MOVES_AHEAD, 4):
            move(g, first)
        for g in range(3):
            move(g, second)
        picked_last = reuse.tile([P, I - MOVE_CUT], U8, name="picked_last", align_bytes=64, offset=960)
        nc.vector.tensor_copy(picked_last[:].bitcast(I32), picked_s[:, second].bitcast(I32))
        nc.sync.dma_start(key_s[96:100, second].bitcast(I32), picked_last[first_row + 12 :, :].bitcast(I32))

        w_src = w_raw[:].rearrange("p j (m t) -> p m j t", t=PACK)
        w_bf = [keep.tile([P, 2, P, PACK], BF16, name="w_bf%d" % pair, align_bytes=64) for pair in range(2)]
        w_dst = [tile[:].rearrange("p t m j -> p m j t") for tile in w_bf]
        nc.vector.tensor_copy(w_dst[0], w_src[:, :, :, :2])
        nc.scalar.copy(w_dst[1], w_src[:, :, :, 2:])
        w_codes = keep.tile([P, C], U32, name="w_codes", align_bytes=64)
        w_scales = keep.tile([P, C], U8, name="w_scales", align_bytes=64)

        def quantise_pair(pair):
            cols = slice(pair * 2 * P, (pair + 1) * 2 * P)
            quantise(w_codes[:, cols], w_scales[:, cols], w_bf[pair][:].rearrange("p t m j -> p (t m j)"))

        quantise_pair(0)
        warm_up(w_codes, w_scales, WARM_AHEAD)

        q_src = q_raw[:].rearrange("p j (c i) -> p c j i", i=4)
        q_bf = [keep.tile([P, P, PACK], BF16, name="q_bf%d" % h, align_bytes=64) for h in range(2)]
        q_dst = [tile[:].rearrange("p (c i) j -> p c j i", i=4) for tile in q_bf]
        cut = Q_SCALAR // 4
        nc.vector.tensor_copy(q_dst[0][:, cut:], q_src[:, cut : P // 4])
        nc.scalar.copy(q_dst[0][:, :cut], q_src[:, :cut])
        nc.scalar.copy(q_dst[1], q_src[:, P // 4 :])
        quantise_pair(1)
        q_scales = [keep.tile([P, P], U8, name="q_scales%d" % h, align_bytes=64) for h in range(2)]
        q_codes = [keep.tile([P, P], U32, name="q_codes%d" % h, align_bytes=64) for h in range(2)]
        for h in range(2):
            quantise(q_codes[h][:], q_scales[h][:], q_bf[h][:].rearrange("p q j -> p (q j)"))

        b_ps = [psum.tile([P, PACK, P], F32, name="b_ps%d" % h) for h in range(2)]
        for h in range(2):
            for t in range(PACK):
                cols = slice(t * P, (t + 1) * P)
                product(b_ps[h][:, t, :], w_codes[:, cols], w_scales[:, cols], q_codes[h][:], q_scales[h][:])
        warm_up(q_codes[1], q_scales[1], WARM_BEHIND)

        b_bf = [keep.tile([P, P, PACK], BF16, name="b_bf%d" % h, align_bytes=64) for h in range(2)]
        b_codes = [keep.tile([P, P], U32, name="b_codes%d" % h, align_bytes=64) for h in range(2)]
        b_scales = [reuse.tile([P, P], U8, name="b_scales%d" % h, align_bytes=64, offset=1024 + P * h) for h in range(2)]
        for h in range(2):
            nc.scalar.copy(b_bf[h][:].rearrange("p (a r) t -> p a r t", r=PACK), b_ps[h][:].rearrange("p t (r a) -> p a r t", r=PACK))

        head = keep.tile([P, HEAD], U32, name="key_head", align_bytes=64)
        rest = reuse.tile([P, I - HEAD], U32, name="key_rest", align_bytes=64, offset=REST_AT)

        def keys(a, b):
            return head[:, a:b] if b <= HEAD else rest[:, a - HEAD : b - HEAD]

        def gather(a, b):
            nc.vector.tensor_copy(keys(a, b), lat_w[:].indirect(offsets[:, a // 16 : b // 16]))

        def quantise_b(h):
            quantise(b_codes[h][:], b_scales[h][:], b_bf[h][:].rearrange("p q t -> p (q t)"))

        gather(0, HEAD)
        quantise_b(0)
        for a, b in GATHERS:
            gather(a, b)
        quantise_b(1)

        early = psum.tile([P, SPLIT], F32, name="scores0_early")
        late = psum.tile([P, I - SPLIT], F32, name="scores0_late")
        scores_1 = psum.tile([P, I], F32, name="scores1")
        for a, b in PASSES_0:
            result = early[:, a:b] if b <= SPLIT else late[:, a - SPLIT : b - SPLIT]
            product(result, b_codes[0][:], b_scales[0][:], keys(a, b), key_s[:, a:b])
        for a, b in PASSES_1:
            product(scores_1[:, a:b], b_codes[1][:], b_scales[1][:], keys(a, b), key_s[:, a:b])

        for h in range(2):
            neg_max = keep.tile([P, 1], F32, name="neg_max%d" % h)
            negated = keep.tile([P, I], F32, name="negated%d" % h)
            p = keep.tile([P, I], F32, name="p%d" % h)
            total = keep.tile([P, 1], F32, name="total%d" % h)
            if h == 0:
                neg_max_early = keep.tile([P, 1], F32, name="neg_max_early")
                nc.vector.tensor_scalar(negated[:, :SPLIT], early[:], -1.0, None, ALU.mult, ALU.min, accum_out=neg_max_early[:])
                nc.vector.tensor_scalar(negated[:, SPLIT:], late[:], -1.0, neg_max_early[:], ALU.mult, ALU.min, accum_out=neg_max[:])
            else:
                nc.vector.tensor_scalar(negated[:], scores_1[:], -1.0, None, ALU.mult, ALU.min, accum_out=neg_max[:])
            nc.scalar.activation(p[:], negated[:], ACT.Exp, bias=neg_max[:], scale=-1.0, accum_out=total[:])
            inv = keep.tile([P, 1], F32, name="inv%d" % h)
            nc.vector.reciprocal(inv[:], total[:])
            y = keep.tile([P, I], F32, name="y%d" % h, align_bytes=256)
            nc.vector.tensor_scalar(y[:], p[:], inv[:], 512.0, ALU.mult, ALU.mult)
            nc.sync.dma_start(out[h * P : (h + 1) * P, :].rearrange("(r a) i -> a r i", r=PACK), y[:])
